import numpy as np
import ml_dtypes


def mxq(x, axis, fmt="e4m3"):
    dtype, down = {"e4m3": (ml_dtypes.float8_e4m3fn, 7), "e5m2": (ml_dtypes.float8_e5m2, 14)}[fmt]
    v = np.moveaxis(np.asarray(x, np.float32).astype(ml_dtypes.bfloat16).astype(np.float64), axis, -1)
    blocks = v.reshape(v.shape[:-1] + (-1, 32))
    amax = np.abs(blocks).max(-1, keepdims=True)
    byte = np.maximum(np.where(amax > 0, np.frexp(amax)[1] - 1 + 127, 0) - down, 1)
    scale = np.exp2(byte - 127.0)
    codes = (blocks / scale).astype(np.float32).astype(dtype).astype(np.float64)
    return np.moveaxis((codes * scale).reshape(v.shape), -1, axis)


WIDE = False


def mx_kscale(k):
    if not WIDE:
        return np.ones(k)
    levels = np.array([10, -10, 5, -5, 0])
    if k % 512:
        return np.exp2(np.random.permutation(np.resize(levels, k // 32))).repeat(32)
    a = np.empty((k // 512, 16))
    for p in range(k // 512):
        a[p, :8] = np.random.permutation(np.resize(levels, 8))
        for g in range(8):
            far = levels[np.abs(levels - a[p, g]) >= 10]
            a[p, g + 8] = far[np.random.randint(len(far))]
    return np.exp2(a.ravel()).repeat(32)


def f64(x):
    return np.asarray(x).astype(np.float64)


def striped(idx):
    return np.tile(np.asarray(idx).reshape(-1, 16).T, (8, 1)).astype(np.uint16)


def unstriped(offs):
    return offs[:16].T.reshape(-1).astype(np.int64)


K, I, U, C, E, O, D = 512, 256, 256, 512, 512, 256, 256


def setup_inputs():
    n = np.random.standard_normal
    idx = np.random.permutation(C)[:I]
    idx2 = np.random.permutation(E)[:U]
    idx3 = np.random.permutation(C)[:O]
    idx4 = np.random.permutation(E)[:D]
    fk = mx_kscale(K)
    return {
        "ca": (np.random.randint(-7, 8, (K, I)).astype(np.float64)).astype(np.float32),
        "cb": (np.random.randint(-7, 8, (K, U)).astype(np.float64)).astype(np.float32),
        "sa": (np.random.uniform(0.1, 0.4, (K, 1)) * fk[:, None]).astype(np.float32),
        "sb": (np.random.uniform(0.01, 0.04, (K, 1)) / fk[:, None]).astype(np.float32),
        "offs": striped(idx),
        "offs2": striped(idx2),
        "offs3": striped(idx3),
        "offs4": striped(idx4),
    }


def reference(ca, cb, sa, sb, offs, offs2, offs3, offs4):
    idx = unstriped(offs)
    idx2 = unstriped(offs2)
    idx3 = unstriped(offs3)
    idx4 = unstriped(offs4)
    pa = np.zeros((K, C))
    pa[:, idx] = f64(ca) * f64(sa)
    pb = np.zeros((K, E))
    pb[:, idx2] = f64(cb) * f64(sb)
    z1 = pa[:, idx3]
    z2 = pb[:, idx4]
    z1q = mxq(z1, 0, "e4m3")
    z2q = mxq(z2, 0, "e4m3")
    y = z1q.T @ z2q
    return y

@@ -1,0 +1,115 @@
+from contextlib import ExitStack
+
+import concourse.mybir as mybir
+
+K, CODES, PAGE, READS = 512, 256, 512, 256
+FLOPS = 2 * K * READS * READS
+
+F32 = mybir.dt.float32
+BF16 = mybir.dt.bfloat16
+U32 = mybir.dt.uint32
+U16 = mybir.dt.uint16
+U8 = mybir.dt.uint8
+FP8X4 = mybir.dt.float8_e4m3fn_x4
+COPY = mybir.ActivationFunctionType.Copy
+
+P = 128
+PACK = 4
+PER_COLUMN = 16
+HALF = 128
+
+
+def tile_list_pagedscores_kernel(tc, ca, cb, sa, sb, offs, offs2, offs3, offs4, out):
+    nc = tc.nc
+    with ExitStack() as ctx:
+        keep = ctx.enter_context(tc.tile_pool(name="keep", bufs=1))
+        psum = ctx.enter_context(tc.psum_pool(name="psum", bufs=1))
+
+        def load_list(src, name):
+            t = keep.tile([P, CODES // PER_COLUMN], U16, name=name)
+            nc.sync.dma_start(t[:], src)
+            return t
+
+        def load_step(src, name):
+            t = keep.tile([P, PACK], F32, name=name)
+            nc.sync.dma_start(t[:], src.rearrange("(p r) o -> p (r o)", r=PACK))
+            return t
+
+        ca_rows = ca.rearrange("(p r) i -> p r i", r=PACK)
+        cb_rows = cb.rearrange("(p r) i -> p r i", r=PACK)
+
+        put_a = load_list(offs, "put_a")
+        step_a = load_step(sa, "step_a")
+        a_first = keep.tile([P, CODES], F32)
+        nc.sync.dma_start(a_first[:], ca_rows[:, 0, :])
+        a_rest = keep.tile([P, PACK - 1, CODES], F32)
+        nc.sync.dma_start(a_rest[:], ca_rows[:, 1:PACK, :])
+        get_a = load_list(offs3, "get_a")
+        put_b = load_list(offs2, "put_b")
+        step_b = load_step(sb, "step_b")
+        b_all = keep.tile([P, PACK, CODES], F32)
+        nc.sync.dma_start(b_all[:], cb_rows)
+        get_b = load_list(offs4, "get_b")
+
+        codes_a = [a_first[:]] + [a_rest[:, r, :] for r in range(PACK - 1)]
+        codes_b = [b_all[:, r, :] for r in range(PACK)]
+
+        pages_a = [keep.tile([P, PAGE], F32, name="page_a%d" % r) for r in range(PACK)]
+        pages_b = [keep.tile([P, PAGE], F32, name="page_b%d" % r) for r in range(PACK)]
+        for page in pages_a + pages_b:
+            nc.vector.memset(page[:], 0.0)
+
+        z1 = keep.tile([P, PACK * READS], BF16, align_bytes=64)
+        z2 = keep.tile([P, PACK * READS], BF16, align_bytes=64)
+        z1_words = keep.tile([P, READS], U32, align_bytes=64)
+        z2_words = keep.tile([P, READS], U32, align_bytes=64)
+        z1_scales = keep.tile([P, READS], U8, align_bytes=64)
+        z2_scales = keep.tile([P, READS], U8, align_bytes=64)
+
+        def put(pages, codes, step, offsets):
+            for r in range(PACK):
+                nc.scalar.activation(
+                    out=pages[r][:].indirect(offsets[:]), in_=codes[r], func=COPY, scale=step[:, r : r + 1]
+                )
+
+        def fetch(z, pages, offsets, c0, c1):
+            for r in range(PACK):
+                nc.scalar.activation(
+                    out=z[:, PACK * c0 + r : PACK * c1 : PACK],
+                    in_=pages[r][:].indirect(offsets[:, c0 // PER_COLUMN : c1 // PER_COLUMN]),
+                    func=COPY,
+                )
+
+        def quantise(words, scales, z, c0, c1):
+            nc.vector.quantize_mx(
+                out=words[:, c0:c1].bitcast(FP8X4), scales=scales[:, c0:c1], in_=z[:, PACK * c0 : PACK * c1]
+            )
+
+        put(pages_a, codes_a, step_a, put_a)
+        fetch(z1, pages_a, get_a, 0, READS)
+        quantise(z1_words, z1_scales, z1, 0, READS)
+        put(pages_b, codes_b, step_b, put_b)
+
+        for d0 in range(0, READS, HALF):
+            d1 = d0 + HALF
+            last = d1 == READS
+            fetch(z2, pages_b, get_b, d0, d1)
+            quantise(z2_words, z2_scales, z2, d0, d1)
+            for o0 in range(0, READS, P):
+                acc = psum.tile([P, HALF], F32, name="acc_%d_%d" % (d0, o0))
+                nc.tensor.matmul_mx(
+                    out=acc[:],
+                    lhsT=z1_words[:, o0 : o0 + P].bitcast(FP8X4),
+                    lhsT_scale=z1_scales[:, o0 : o0 + P],
+                    rhs=z2_words[:, d0:d1].bitcast(FP8X4),
+                    rhs_scale=z2_scales[:, d0:d1],
+                    start=True,
+                    stop=True,
+                )
+                res = keep.tile([P, HALF], F32, name="res_%d_%d" % (d0, o0))
+                if last and o0 > 0:
+                    nc.scalar.copy(out=res[:], in_=acc[:])
+                    nc.scalar.dma_start(out[o0 : o0 + P, d0:d1], res[:])
+                else:
+                    nc.vector.tensor_copy(out=res[:], in_=acc[:])
+                    nc.sync.dma_start(out[o0 : o0 + P, d0:d1], res[:])

@@ -35,6 +35,11 @@ def tile_list_pagedscores_kernel(tc, ca, cb, sa, sb, offs, offs2, offs3, offs4, 
             nc.sync.dma_start(t[:], src.rearrange("(p r) o -> p (r o)", r=PACK))
             return t
 
+        warm_in = keep.tile([P, 1], F32)
+        warm_out = keep.tile([P, 1], F32)
+        nc.vector.memset(warm_in[:], 0.0)
+        nc.scalar.activation(out=warm_out[:], in_=warm_in[:], func=COPY)
+
         ca_rows = ca.rearrange("(p r) i -> p r i", r=PACK)
         cb_rows = cb.rearrange("(p r) i -> p r i", r=PACK)
 

@@ -30,9 +30,9 @@ def tile_list_pagedscores_kernel(tc, ca, cb, sa, sb, offs, offs2, offs3, offs4, 
             nc.sync.dma_start(t[:], src)
             return t
 
-        def load_step(src, name):
+        def load_step(src, name, queue):
             t = keep.tile([P, PACK], F32, name=name)
-            nc.sync.dma_start(t[:], src.rearrange("(p r) o -> p (r o)", r=PACK))
+            queue.dma_start(t[:], src.rearrange("(p r) o -> p (r o)", r=PACK))
             return t
 
         warm_in = keep.tile([P, 1], F32)
@@ -43,15 +43,15 @@ def tile_list_pagedscores_kernel(tc, ca, cb, sa, sb, offs, offs2, offs3, offs4, 
         ca_rows = ca.rearrange("(p r) i -> p r i", r=PACK)
         cb_rows = cb.rearrange("(p r) i -> p r i", r=PACK)
 
-        put_a = load_list(offs, "put_a")
-        step_a = load_step(sa, "step_a")
         a_first = keep.tile([P, CODES], F32)
         nc.sync.dma_start(a_first[:], ca_rows[:, 0, :])
+        put_a = load_list(offs, "put_a")
+        step_a = load_step(sa, "step_a", nc.sync)
         a_rest = keep.tile([P, PACK - 1, CODES], F32)
         nc.sync.dma_start(a_rest[:], ca_rows[:, 1:PACK, :])
         get_a = load_list(offs3, "get_a")
         put_b = load_list(offs2, "put_b")
-        step_b = load_step(sb, "step_b")
+        step_b = load_step(sb, "step_b", nc.sync)
         b_all = keep.tile([P, PACK, CODES], F32)
         nc.sync.dma_start(b_all[:], cb_rows)
         get_b = load_list(offs4, "get_b")
@@ -95,13 +95,11 @@ def tile_list_pagedscores_kernel(tc, ca, cb, sa, sb, offs, offs2, offs3, offs4, 
         quantise(z1_words, z1_scales, z1, 0, READS)
         put(pages_b, codes_b, step_b, put_b)
 
-        for d0 in range(0, READS, HALF):
-            d1 = d0 + HALF
-            last = d1 == READS
-            fetch(z2, pages_b, get_b, d0, d1)
+        def score(d0, d1):
             quantise(z2_words, z2_scales, z2, d0, d1)
+            accs = []
             for o0 in range(0, READS, P):
-                acc = psum.tile([P, HALF], F32, name="acc_%d_%d" % (d0, o0))
+                acc = psum.tile([P, d1 - d0], F32, name="acc_%d_%d" % (d0, o0))
                 nc.tensor.matmul_mx(
                     out=acc[:],
                     lhsT=z1_words[:, o0 : o0 + P].bitcast(FP8X4),
@@ -111,10 +109,21 @@ def tile_list_pagedscores_kernel(tc, ca, cb, sa, sb, offs, offs2, offs3, offs4, 
                     start=True,
                     stop=True,
                 )
-                res = keep.tile([P, HALF], F32, name="res_%d_%d" % (d0, o0))
-                if last and o0 > 0:
+                accs.append(acc)
+            return accs
+
+        def store(accs, d0, d1, last):
+            for h, acc in enumerate(accs):
+                res = keep.tile([P, d1 - d0], F32, name="res_%d_%d" % (d0, h))
+                if last and h > 0:
                     nc.scalar.copy(out=res[:], in_=acc[:])
-                    nc.scalar.dma_start(out[o0 : o0 + P, d0:d1], res[:])
+                    nc.scalar.dma_start(out[h * P : (h + 1) * P, d0:d1], res[:])
                 else:
                     nc.vector.tensor_copy(out=res[:], in_=acc[:])
-                    nc.sync.dma_start(out[o0 : o0 + P, d0:d1], res[:])
+                    nc.sync.dma_start(out[h * P : (h + 1) * P, d0:d1], res[:])
+
+        fetch(z2, pages_b, get_b, 0, 192)
+        store(score(0, 128), 0, 128, False)
+        store(score(128, 192), 128, 192, False)
+        fetch(z2, pages_b, get_b, 192, 256)
+        store(score(192, 256), 192, 256, True)

@@ -43,12 +43,16 @@ def tile_list_pagedscores_kernel(tc, ca, cb, sa, sb, offs, offs2, offs3, offs4, 
         ca_rows = ca.rearrange("(p r) i -> p r i", r=PACK)
         cb_rows = cb.rearrange("(p r) i -> p r i", r=PACK)
 
-        a_first = keep.tile([P, CODES], F32)
-        nc.sync.dma_start(a_first[:], ca_rows[:, 0, :])
+        a_head = keep.tile([P, 64], F32)
+        nc.sync.dma_start(a_head[:], ca_rows[:, 0, 0:64])
         put_a = load_list(offs, "put_a")
         step_a = load_step(sa, "step_a", nc.sync)
-        a_rest = keep.tile([P, PACK - 1, CODES], F32)
-        nc.sync.dma_start(a_rest[:], ca_rows[:, 1:PACK, :])
+        a_second = keep.tile([P, CODES], F32)
+        nc.sync.dma_start(a_second[:], ca_rows[:, 1, :])
+        a_first = keep.tile([P, CODES - 64], F32)
+        nc.sync.dma_start(a_first[:], ca_rows[:, 0, 64:CODES])
+        a_rest = keep.tile([P, PACK - 2, CODES], F32)
+        nc.sync.dma_start(a_rest[:], ca_rows[:, 2:PACK, :])
         get_a = load_list(offs3, "get_a")
         put_b = load_list(offs2, "put_b")
         step_b = load_step(sb, "step_b", nc.sync)
@@ -56,7 +60,6 @@ def tile_list_pagedscores_kernel(tc, ca, cb, sa, sb, offs, offs2, offs3, offs4, 
         nc.sync.dma_start(b_all[:], cb_rows)
         get_b = load_list(offs4, "get_b")
 
-        codes_a = [a_first[:]] + [a_rest[:, r, :] for r in range(PACK - 1)]
         codes_b = [b_all[:, r, :] for r in range(PACK)]
 
         pages_a = [keep.tile([P, PAGE], F32, name="page_a%d" % r) for r in range(PACK)]
@@ -90,7 +93,19 @@ def tile_list_pagedscores_kernel(tc, ca, cb, sa, sb, offs, offs2, offs3, offs4, 
                 out=words[:, c0:c1].bitcast(FP8X4), scales=scales[:, c0:c1], in_=z[:, PACK * c0 : PACK * c1]
             )
 
-        put(pages_a, codes_a, step_a, put_a)
+        def put_part(r, src, c0, c1):
+            nc.scalar.activation(
+                out=pages_a[r][:].indirect(put_a[:, c0 // PER_COLUMN : c1 // PER_COLUMN]),
+                in_=src,
+                func=COPY,
+                scale=step_a[:, r : r + 1],
+            )
+
+        put_part(0, a_head[:], 0, 64)
+        put_part(1, a_second[:], 0, CODES)
+        put_part(0, a_first[:], 64, CODES)
+        put_part(2, a_rest[:, 0, :], 0, CODES)
+        put_part(3, a_rest[:, 1, :], 0, CODES)
         fetch(z1, pages_a, get_a, 0, READS)
         quantise(z1_words, z1_scales, z1, 0, READS)
         put(pages_b, codes_b, step_b, put_b)
@@ -122,8 +137,6 @@ def tile_list_pagedscores_kernel(tc, ca, cb, sa, sb, offs, offs2, offs3, offs4, 
                     nc.vector.tensor_copy(out=res[:], in_=acc[:])
                     nc.sync.dma_start(out[h * P : (h + 1) * P, d0:d1], res[:])
 
-        fetch(z2, pages_b, get_b, 0, 192)
-        store(score(0, 128), 0, 128, False)
-        store(score(128, 192), 128, 192, False)
-        fetch(z2, pages_b, get_b, 192, 256)
-        store(score(192, 256), 192, 256, True)
+        for d0, d1 in ((0, 128), (128, 192), (192, 256)):
+            fetch(z2, pages_b, get_b, d0, d1)
+            store(score(d0, d1), d0, d1, d1 == READS)

from contextlib import ExitStack

import concourse.mybir as mybir

K, CODES, PAGE, READS = 512, 256, 512, 256
FLOPS = 2 * K * READS * READS

F32 = mybir.dt.float32
BF16 = mybir.dt.bfloat16
U32 = mybir.dt.uint32
U16 = mybir.dt.uint16
U8 = mybir.dt.uint8
FP8X4 = mybir.dt.float8_e4m3fn_x4
COPY = mybir.ActivationFunctionType.Copy

P = 128
PACK = 4
PER_COLUMN = 16
HALF = 128


def tile_list_pagedscores_kernel(tc, ca, cb, sa, sb, offs, offs2, offs3, offs4, out):
    nc = tc.nc
    with ExitStack() as ctx:
        keep = ctx.enter_context(tc.tile_pool(name="keep", bufs=1))
        psum = ctx.enter_context(tc.psum_pool(name="psum", bufs=1))

        def load_list(src, name):
            t = keep.tile([P, CODES // PER_COLUMN], U16, name=name)
            nc.sync.dma_start(t[:], src)
            return t

        def load_step(src, name, queue):
            t = keep.tile([P, PACK], F32, name=name)
            queue.dma_start(t[:], src.rearrange("(p r) o -> p (r o)", r=PACK))
            return t

        warm_in = keep.tile([P, 1], F32)
        warm_out = keep.tile([P, 1], F32)
        nc.vector.memset(warm_in[:], 0.0)
        nc.scalar.activation(out=warm_out[:], in_=warm_in[:], func=COPY)

        ca_rows = ca.rearrange("(p r) i -> p r i", r=PACK)
        cb_rows = cb.rearrange("(p r) i -> p r i", r=PACK)

        a_head = keep.tile([P, 64], F32)
        nc.sync.dma_start(a_head[:], ca_rows[:, 0, 0:64])
        put_a = load_list(offs, "put_a")
        step_a = load_step(sa, "step_a", nc.sync)
        a_second = keep.tile([P, CODES], F32)
        nc.sync.dma_start(a_second[:], ca_rows[:, 1, :])
        a_first = keep.tile([P, CODES - 64], F32)
        nc.sync.dma_start(a_first[:], ca_rows[:, 0, 64:CODES])
        a_rest = keep.tile([P, PACK - 2, CODES], F32)
        nc.sync.dma_start(a_rest[:], ca_rows[:, 2:PACK, :])
        get_a = load_list(offs3, "get_a")
        put_b = load_list(offs2, "put_b")
        step_b = load_step(sb, "step_b", nc.sync)
        b_all = keep.tile([P, PACK, CODES], F32)
        nc.sync.dma_start(b_all[:], cb_rows)
        get_b = load_list(offs4, "get_b")

        codes_b = [b_all[:, r, :] for r in range(PACK)]

        pages_a = [keep.tile([P, PAGE], F32, name="page_a%d" % r) for r in range(PACK)]
        pages_b = [keep.tile([P, PAGE], F32, name="page_b%d" % r) for r in range(PACK)]
        for page in pages_a + pages_b:
            nc.vector.memset(page[:], 0.0)

        z1 = keep.tile([P, PACK * READS], BF16, align_bytes=64)
        z2 = keep.tile([P, PACK * READS], BF16, align_bytes=64)
        z1_words = keep.tile([P, READS], U32, align_bytes=64)
        z2_words = keep.tile([P, READS], U32, align_bytes=64)
        z1_scales = keep.tile([P, READS], U8, align_bytes=64)
        z2_scales = keep.tile([P, READS], U8, align_bytes=64)

        def put(pages, codes, step, offsets):
            for r in range(PACK):
                nc.scalar.activation(
                    out=pages[r][:].indirect(offsets[:]), in_=codes[r], func=COPY, scale=step[:, r : r + 1]
                )

        def fetch(z, pages, offsets, c0, c1):
            for r in range(PACK):
                nc.scalar.activation(
                    out=z[:, PACK * c0 + r : PACK * c1 : PACK],
                    in_=pages[r][:].indirect(offsets[:, c0 // PER_COLUMN : c1 // PER_COLUMN]),
                    func=COPY,
                )

        def quantise(words, scales, z, c0, c1):
            nc.vector.quantize_mx(
                out=words[:, c0:c1].bitcast(FP8X4), scales=scales[:, c0:c1], in_=z[:, PACK * c0 : PACK * c1]
            )

        def put_part(r, src, c0, c1):
            nc.scalar.activation(
                out=pages_a[r][:].indirect(put_a[:, c0 // PER_COLUMN : c1 // PER_COLUMN]),
                in_=src,
                func=COPY,
                scale=step_a[:, r : r + 1],
            )

        put_part(0, a_head[:], 0, 64)
        put_part(1, a_second[:], 0, CODES)
        put_part(0, a_first[:], 64, CODES)
        put_part(2, a_rest[:, 0, :], 0, CODES)
        put_part(3, a_rest[:, 1, :], 0, CODES)
        fetch(z1, pages_a, get_a, 0, READS)
        quantise(z1_words, z1_scales, z1, 0, READS)
        put(pages_b, codes_b, step_b, put_b)

        def score(d0, d1):
            quantise(z2_words, z2_scales, z2, d0, d1)
            accs = []
            for o0 in range(0, READS, P):
                acc = psum.tile([P, d1 - d0], F32, name="acc_%d_%d" % (d0, o0))
                nc.tensor.matmul_mx(
                    out=acc[:],
                    lhsT=z1_words[:, o0 : o0 + P].bitcast(FP8X4),
                    lhsT_scale=z1_scales[:, o0 : o0 + P],
                    rhs=z2_words[:, d0:d1].bitcast(FP8X4),
                    rhs_scale=z2_scales[:, d0:d1],
                    start=True,
                    stop=True,
                )
                accs.append(acc)
            return accs

        def store(accs, d0, d1, last):
            for h, acc in enumerate(accs):
                res = keep.tile([P, d1 - d0], F32, name="res_%d_%d" % (d0, h))
                if last and h > 0:
                    nc.scalar.copy(out=res[:], in_=acc[:])
                    nc.scalar.dma_start(out[h * P : (h + 1) * P, d0:d1], res[:])
                else:
                    nc.vector.tensor_copy(out=res[:], in_=acc[:])
                    nc.sync.dma_start(out[h * P : (h + 1) * P, d0:d1], res[:])

        for d0, d1 in ((0, 128), (128, 192), (192, 256)):
            fetch(z2, pages_b, get_b, d0, d1)
            store(score(d0, d1), d0, d1, d1 == READS)
